import numpy as np
import ml_dtypes


def mxq(x, axis, fmt="e4m3"):
    dtype, down = {"e4m3": (ml_dtypes.float8_e4m3fn, 7), "e5m2": (ml_dtypes.float8_e5m2, 14)}[fmt]
    v = np.moveaxis(np.asarray(x, np.float32).astype(ml_dtypes.bfloat16).astype(np.float64), axis, -1)
    blocks = v.reshape(v.shape[:-1] + (-1, 32))
    amax = np.abs(blocks).max(-1, keepdims=True)
    byte = np.maximum(np.where(amax > 0, np.frexp(amax)[1] - 1 + 127, 0) - down, 1)
    scale = np.exp2(byte - 127.0)
    codes = (blocks / scale).astype(np.float32).astype(dtype).astype(np.float64)
    return np.moveaxis((codes * scale).reshape(v.shape), -1, axis)


WIDE = False


def mx_kscale(k):
    if not WIDE:
        return np.ones(k)
    levels = np.array([24, -24, 12, -12, 0])
    if k % 512:
        return np.exp2(np.random.permutation(np.resize(levels, k // 32))).repeat(32)
    a = np.empty((k // 512, 16))
    for p in range(k // 512):
        a[p, :8] = np.random.permutation(np.resize(levels, 8))
        for g in range(8):
            far = levels[np.abs(levels - a[p, g]) >= 10]
            a[p, g + 8] = far[np.random.randint(len(far))]
    return np.exp2(a.ravel()).repeat(32)


def f64(x):
    return np.asarray(x).astype(np.float64)


E2M1 = np.array([0.0, 0.5, 1.0, 1.5, 2.0, 3.0, 4.0, 6.0, -0.0, -0.5, -1.0, -1.5, -2.0, -3.0, -4.0, -6.0])


def pack_weight(w, fmt):
    k, n = w.shape
    w = f64(np.asarray(w, np.float32).astype(ml_dtypes.bfloat16)).reshape(k // 32, 32, n)
    amax = np.abs(w).max(1)
    if fmt == "e4m3":
        byte = np.frexp(amax)[1] - 1 + 127 - 7
    else:
        mant, ex = np.frexp(amax / 6.0)
        byte = np.where(mant > 0.5, ex, ex - 1) + 127
    byte = np.clip(np.where(amax > 0, byte, 1), 1, 254)
    scaled = (w * np.exp2(127.0 - byte)[:, None, :]).reshape(k, n).astype(np.float32)
    by_word = np.ascontiguousarray(scaled.reshape(k // 512, 128, 4, n).transpose(0, 1, 3, 2))
    if fmt == "e4m3":
        words = by_word.astype(ml_dtypes.float8_e4m3fn).view(np.uint8)
    else:
        c = by_word.astype(ml_dtypes.float4_e2m1fn).view(np.uint8) & 0xF
        words = (c[..., 0::2] | (c[..., 1::2] << 4)).reshape(k // 512, 128, 2 * n)
    return np.ascontiguousarray(words), np.ascontiguousarray(byte.astype(np.uint8).reshape(k // 512, 16, n))


def unpack_weight(words, scales, fmt):
    g, _, n = scales.shape
    words = np.ascontiguousarray(words).reshape(g, 128, n, -1)
    if fmt == "e4m3":
        vals = words.view(ml_dtypes.float8_e4m3fn).astype(np.float64)
    else:
        nib = np.empty((g, 128, n, 4), np.uint8)
        nib[..., 0::2] = words & 0xF
        nib[..., 1::2] = words >> 4
        vals = E2M1[nib]
    vals = vals * np.repeat(np.exp2(scales.astype(np.float64) - 127.0), 8, axis=1)[..., None]
    return vals.transpose(0, 1, 3, 2).reshape(g * 512, n)


K, N, T = 512, 512, 512


def setup_inputs():
    n = np.random.standard_normal
    s = mx_kscale(K)[:, None]
    p_wr = pack_weight(n((K, N)) / np.sqrt(4 * K) / s, "e2m1")
    p_wi = pack_weight(n((K, N)) / np.sqrt(4 * K) / s, "e4m3")
    p_wj = pack_weight(n((K, N)) / np.sqrt(4 * K) / s, "e4m3")
    p_wk = pack_weight(n((K, N)) / np.sqrt(4 * K) / s, "e4m3")
    return {
        "xr": (n((K, T)) * s).astype(np.float32),
        "xi": (n((K, T)) * s).astype(np.float32),
        "xj": (n((K, T)) * s).astype(np.float32),
        "xk": (n((K, T)) * s).astype(np.float32),
        "wr_words": p_wr[0],
        "wr_scales": p_wr[1],
        "wi_words": p_wi[0],
        "wi_scales": p_wi[1],
        "wj_words": p_wj[0],
        "wj_scales": p_wj[1],
        "wk_words": p_wk[0],
        "wk_scales": p_wk[1],
    }


def reference(xr, xi, xj, xk, wr_words, wr_scales, wi_words, wi_scales, wj_words, wj_scales, wk_words, wk_scales):
    xr_ = mxq(f64(xr), 0, "e4m3")
    xi_ = mxq(f64(xi), 0, "e4m3")
    xj_ = mxq(f64(xj), 0, "e4m3")
    xk_ = mxq(f64(xk), 0, "e4m3")
    wr_ = unpack_weight(wr_words, wr_scales, "e2m1")
    wi_ = unpack_weight(wi_words, wi_scales, "e4m3")
    wj_ = unpack_weight(wj_words, wj_scales, "e4m3")
    wk_ = unpack_weight(wk_words, wk_scales, "e4m3")
    pr = wr_.T @ xr_
    mr = wi_.T @ xi_ + wj_.T @ xj_ + wk_.T @ xk_
    pi = wr_.T @ xi_ + wi_.T @ xr_ + wj_.T @ xk_
    mi = wk_.T @ xj_
    pj = wr_.T @ xj_ + wj_.T @ xr_ + wk_.T @ xi_
    mj = wi_.T @ xk_
    pk = wr_.T @ xk_ + wi_.T @ xj_ + wk_.T @ xr_
    mk = wj_.T @ xi_
    return np.maximum(pr - mr, 0.0), np.maximum(pi - mi, 0.0), np.maximum(pj - mj, 0.0), np.maximum(pk - mk, 0.0)

@@ -1,0 +1,346 @@
+from contextlib import ExitStack
+
+import concourse.mybir as mybir
+
+K, N, T = 512, 512, 512
+FLOPS = 16 * 2 * K * N * T
+
+F32 = mybir.dt.float32
+BF16 = mybir.dt.bfloat16
+I32 = mybir.dt.int32
+U32 = mybir.dt.uint32
+U8 = mybir.dt.uint8
+FP8X4 = mybir.dt.float8_e4m3fn_x4
+FP4X4 = mybir.dt.float4_e2m1fn_x4
+ALU = mybir.AluOpType
+ACT = mybir.ActivationFunctionType
+
+P = 128
+PACK = 4
+HALF = T // 2
+BANK = 512
+F32_MAX = 3.4028234663852886e38
+SLOT = {"r": 0, "k": 1, "i": 2, "j": 3}
+LEFT = slice(0, HALF)
+RIGHT = slice(HALF, BANK)
+WHOLE = slice(0, BANK)
+
+
+def tile_mix_quat_relu_kernel(
+    tc, xr, xi, xj, xk, wr_words, wr_scales, wi_words, wi_scales, wj_words, wj_scales, wk_words, wk_scales,
+    out_0, out_1, out_2, out_3,
+):
+    nc = tc.nc
+    x_hbm = {"r": xr, "i": xi, "j": xj, "k": xk}
+    words_hbm = {
+        "r": wr_words[0],
+        "i": wi_words[0].rearrange("p n t -> p (n t)"),
+        "j": wj_words[0].rearrange("p n t -> p (n t)"),
+        "k": wk_words[0].rearrange("p n t -> p (n t)"),
+    }
+    scales_hbm = {"r": wr_scales[0], "i": wi_scales[0], "j": wj_scales[0], "k": wk_scales[0]}
+    out_hbm = {"r": out_0, "i": out_1, "j": out_2, "k": out_3}
+
+    with ExitStack() as ctx:
+        sb = ctx.enter_context(tc.tile_pool(name="sb", bufs=1))
+        ps = ctx.enter_context(tc.psum_pool(name="ps", bufs=1))
+        ctx.enter_context(tc.manual_schedule())
+
+        bank = [ps.tile([P, BANK], F32, name="bank%d" % b) for b in range(8)]
+        w_codes = {}
+        w_scales = {}
+        for c in "rijk":
+            w_codes[c] = sb.tile([P, N * (2 if c == "r" else 4)], U8, name="w_codes_" + c, align_bytes=64)
+            w_scales[c] = sb.tile([P, N], U8, name="w_scales_" + c, align_bytes=64)
+        x_codes = [sb.tile([P, 4 * HALF], U32, name="x_codes%d" % h, align_bytes=64) for h in range(2)]
+        x_scales = [sb.tile([P, 4 * HALF], U8, name="x_scales%d" % h, align_bytes=64) for h in range(2)]
+        raw = {}
+        grouped = {}
+
+        def load_x(c, h):
+            raw[c, h] = sb.tile([P, PACK, HALF], F32, name="raw_%s%d" % (c, h))
+            cols = x_hbm[c][:, h * HALF : (h + 1) * HALF]
+            nc.sync.dma_start(out=raw[c, h][:], in_=cols.rearrange("(p j) t -> p j t", j=PACK))
+
+        def load_words(c):
+            nc.sync.dma_start(out=w_codes[c][:].bitcast(I32), in_=words_hbm[c].bitcast(I32))
+
+        def load_scales(c):
+            for q in range(4):
+                nc.sync.dma_start(
+                    out=w_scales[c][32 * q : 32 * q + 4, :].bitcast(I32),
+                    in_=scales_hbm[c][4 * q : 4 * q + 4, :].bitcast(I32),
+                )
+
+        def interleave(c, h, on_scalar=False):
+            grouped[c, h] = sb.tile([P, PACK * HALF], BF16, name="grouped_%s%d" % (c, h), align_bytes=64)
+            dst = grouped[c, h][:].rearrange("p (c i j) -> p c j i", i=2, j=PACK)
+            src = raw[c, h][:].rearrange("p j (c i) -> p c j i", i=2)
+            if on_scalar:
+                nc.scalar.copy(out=dst, in_=src)
+            else:
+                nc.vector.tensor_copy(out=dst, in_=src)
+
+        def quantize(c, h):
+            cols = slice(SLOT[c] * HALF, (SLOT[c] + 1) * HALF)
+            nc.vector.quantize_mx(out=x_codes[h][:, cols].bitcast(FP8X4), scales=x_scales[h][:, cols], in_=grouped[c, h][:])
+
+        def mm(b, cols, w, n, x, h, start=False, stop=False, skip=0):
+            width = cols.stop - cols.start
+            x0 = SLOT[x] * HALF + skip
+            if w == "r":
+                lhs = w_codes[w][:, 2 * P * n : 2 * P * (n + 1)].bitcast(FP4X4)
+            else:
+                lhs = w_codes[w][:, 4 * P * n : 4 * P * (n + 1)].bitcast(FP8X4)
+            nc.tensor.matmul_mx(
+                out=bank[b][:, cols],
+                lhsT=lhs,
+                lhsT_scale=w_scales[w][:, P * n : P * (n + 1)],
+                rhs=x_codes[h][:, x0 : x0 + width].bitcast(FP8X4),
+                rhs_scale=x_scales[h][:, x0 : x0 + width],
+                start=start,
+                stop=stop,
+            )
+
+        def lone_pair(b, w, n0, x, h):
+            mm(b, LEFT, w, n0, x, h, True, True)
+            mm(b, RIGHT, w, n0 + 1, x, h, True, True)
+
+        def hold(dst, b, cols=WHOLE):
+            src = bank[b][:, cols]
+            if len(dst.shape) == 3:
+                src = src.rearrange("p (a t) -> p a t", a=2)
+            nc.scalar.activation(out=dst, in_=src, func=ACT.Copy)
+
+        def new(name, width=BANK):
+            fresh = sb.tile([P, width], F32, name=name)
+            return fresh
+
+        def sub(dst, plus, minus):
+            nc.vector.tensor_tensor(out=dst, in0=plus, in1=minus, op=ALU.subtract)
+
+        def relu(dst, src, eng):
+            if eng == "s":
+                nc.scalar.activation(out=dst, in_=src, func=ACT.Relu)
+            elif eng == "g":
+                nc.gpsimd.tensor_scalar(out=dst, in0=src, scalar1=F32_MAX, scalar2=0.0, op0=ALU.min, op1=ALU.max)
+            else:
+                nc.vector.tensor_scalar_max(out=dst, in0=src, scalar1=0.0)
+
+        def store(c, n, h, src):
+            nc.sync.dma_start(out=out_hbm[c][P * n : P * (n + 1), h * HALF : (h + 1) * HALF], in_=src)
+
+        def store_pair(c, n0, h, src):
+            rows = out_hbm[c][P * n0 : P * (n0 + 2), h * HALF : (h + 1) * HALF]
+            nc.sync.dma_start(out=rows.rearrange("(a p) t -> p a t", p=P), in_=src)
+
+        for c in "rijk":
+            nc.vector.memset(w_scales[c][:].bitcast(I32), 0)
+        load_x("r", 0)
+        load_words("r")
+        load_scales("r")
+        load_words("i")
+        load_words("j")
+        load_scales("i")
+        load_x("i", 0)
+        load_scales("j")
+        load_words("k")
+        load_x("j", 0)
+        load_scales("k")
+        load_x("k", 0)
+        for c in "rijk":
+            load_x(c, 1)
+
+        C = [0, 1, 2, 3]
+        KB = [4, 5]
+        L = [6, 7]
+        held_pr = [new("held_pr%d" % a) for a in range(2)]
+        held_mk = [new("held_mk%d" % a) for a in range(2)]
+        held_mij = [sb.tile([P, 2, 2, HALF], F32, name="held_mij%d" % a) for a in range(2)]
+
+        interleave("r", 0)
+        quantize("r", 0)
+        for a in range(2):
+            lone_pair(L[a], "r", 2 * a, "r", 0)
+            hold(held_pr[a][:], L[a])
+        for n in range(4):
+            mm(C[n], LEFT, "i", n, "r", 0, start=True)
+        for n in range(4):
+            mm(C[n], RIGHT, "j", n, "r", 0)
+        interleave("i", 0)
+        quantize("i", 0)
+        for a in range(2):
+            lone_pair(L[a], "j", 2 * a, "i", 0)
+            hold(held_mk[a][:], L[a])
+        for a in range(2):
+            mm(KB[a], LEFT, "k", 2 * a, "r", 0, start=True)
+            mm(KB[a], RIGHT, "k", 2 * a + 1, "r", 0)
+        for n in range(4):
+            mm(C[n], RIGHT, "k", n, "i", 0)
+        interleave("j", 0)
+        quantize("j", 0)
+        for a in range(2):
+            lone_pair(L[a], "k", 2 * a, "j", 0)
+            hold(held_mij[a][:, :, 0, :], L[a])
+        for a in range(2):
+            mm(KB[a], LEFT, "i", 2 * a, "j", 0)
+            mm(KB[a], RIGHT, "i", 2 * a + 1, "j", 0)
+        interleave("k", 0)
+        quantize("k", 0)
+        for a in range(2):
+            lone_pair(L[a], "i", 2 * a, "k", 0)
+            if a == 1:
+                interleave("i", 1, on_scalar=True)
+            hold(held_mij[a][:, :, 1, :], L[a])
+            for n in (2 * a, 2 * a + 1):
+                mm(C[n], WHOLE, "r", n, "i", 0)
+                mm(C[n], LEFT, "j", n, "k", 0, stop=True)
+        for a in range(2):
+            for q in range(4):
+                mm(KB[a], slice(P * q, P * (q + 1)), "r", 2 * a + q // 2, "k", 0, stop=(q == 3), skip=P * (q % 2))
+        for a in range(2):
+            for side, n in ((LEFT, 2 * a), (RIGHT, 2 * a + 1)):
+                mm(L[a], side, "i", n, "i", 0, start=True)
+                mm(L[a], side, "j", n, "j", 0)
+                mm(L[a], side, "k", n, "k", 0, stop=True)
+
+        diff_c = [new("diff_c%d" % n) for n in range(4)]
+        res_c = [sb.tile([P, 2, 2, HALF], F32, name="res_c%d" % a) for a in range(2)]
+        diff_k = [new("diff_k%d" % a) for a in range(2)]
+        res_k = [new("res_k%d" % a) for a in range(2)]
+        diff_r = [new("diff_r%d" % a) for a in range(2)]
+        res_r = [new("res_r%d" % a) for a in range(2)]
+
+        def flat(ap):
+            return ap.rearrange("p a t -> p (a t)")
+
+        def pair(ap):
+            return ap.rearrange("p (a t) -> p a t", a=2)
+
+        def sub_c(n):
+            sub(diff_c[n][:], bank[C[n]][:], flat(held_mij[n // 2][:, n % 2, :, :]))
+
+        def relu_c(n, eng):
+            relu(flat(res_c[n // 2][:, n % 2, :, :]), diff_c[n][:], eng)
+
+        def store_c(a):
+            store_pair("i", 2 * a, 0, res_c[a][:, :, 0, :])
+            store_pair("j", 2 * a, 0, res_c[a][:, :, 1, :])
+
+        def finish_k(a, eng):
+            relu(res_k[a][:], diff_k[a][:], eng)
+            store_pair("k", 2 * a, 0, pair(res_k[a][:]))
+
+        def finish_r(a, eng):
+            relu(res_r[a][:], diff_r[a][:], eng)
+            store_pair("r", 2 * a, 0, pair(res_r[a][:]))
+
+        interleave("r", 1)
+        quantize("r", 1)
+        sub_c(0)
+        sub_c(1)
+        relu_c(0, "v")
+        interleave("j", 1, on_scalar=True)
+        relu_c(1, "s")
+        store_c(0)
+        quantize("i", 1)
+        sub_c(2)
+        relu_c(2, "s")
+        interleave("k", 1)
+        quantize("j", 1)
+        quantize("k", 1)
+        sub_c(3)
+        relu_c(3, "g")
+        store_c(1)
+        for a in range(2):
+            sub(diff_k[a][:], bank[KB[a]][:], held_mk[a][:])
+        for a in range(2):
+            sub(diff_r[a][:], held_pr[a][:], bank[L[a]][:])
+
+        def group_c(b, n):
+            mm(b, LEFT, "i", n, "r", 1, start=True)
+            mm(b, RIGHT, "j", n, "r", 1)
+            mm(b, RIGHT, "k", n, "i", 1)
+            mm(b, WHOLE, "r", n, "i", 1)
+            mm(b, LEFT, "j", n, "k", 1, stop=True)
+
+        def group_d(b, n):
+            mm(b, LEFT, "k", n, "j", 1, True, True)
+            mm(b, RIGHT, "i", n, "k", 1, True, True)
+
+        def group_a(b, n):
+            mm(b, WHOLE, "r", n, "r", 1, start=True)
+            mm(b, RIGHT, "i", n, "j", 1)
+            mm(b, RIGHT, "k", n, "r", 1, stop=True)
+
+        def group_mk(b, n):
+            mm(b, RIGHT, "j", n, "i", 1, True, True)
+
+        def group_mr(b, n):
+            mm(b, LEFT, "i", n, "i", 1, start=True)
+            mm(b, LEFT, "j", n, "j", 1)
+            mm(b, LEFT, "k", n, "k", 1, stop=True)
+
+        held_d = [new("held_d%d" % n) for n in range(4)]
+        held_a = [new("held_a%d" % n) for n in range(4)]
+        diff_cd = [new("diff_cd%d" % n) for n in range(4)]
+        res_cd = [new("res_cd%d" % n) for n in range(4)]
+        diff_ab = [new("diff_ab%d" % n) for n in range(4)]
+        res_ab = [new("res_ab%d" % n) for n in range(4)]
+
+        def finish_cd(n, eng):
+            relu(res_cd[n][:], diff_cd[n][:], eng)
+            store("i", n, 1, res_cd[n][:, LEFT])
+            store("j", n, 1, res_cd[n][:, RIGHT])
+
+        def finish_ab(n, eng):
+            relu(res_ab[n][:], diff_ab[n][:], eng)
+            store("r", n, 1, res_ab[n][:, LEFT])
+            store("k", n, 1, res_ab[n][:, RIGHT])
+
+        def bda(n, bb, bd, ba):
+            group_mk(bb, n)
+            group_mr(bb, n)
+            hold(held_a[n][:], bb)
+            group_d(bd, n)
+            hold(held_d[n][:], bd)
+            group_a(ba, n)
+
+        def sub_ab(n, ba):
+            sub(diff_ab[n][:], bank[ba][:], held_a[n][:])
+
+        bda(0, 0, 1, 2)
+        finish_k(0, "g")
+        finish_k(1, "s")
+        finish_r(0, "g")
+        finish_r(1, "g")
+        sub_ab(0, 2)
+        bda(1, 3, 0, 4)
+        finish_ab(0, "g")
+        sub_ab(1, 4)
+        finish_ab(1, "g")
+        bda(2, 1, 5, 6)
+        sub_ab(2, 6)
+        finish_ab(2, "g")
+        bda(3, 7, 2, 3)
+        sub_ab(3, 3)
+        finish_ab(3, "s")
+        for n, b in ((0, 0), (1, 4), (2, 1)):
+            group_c(b, n)
+            if n < 2:
+                sub(diff_cd[n][:], bank[b][:], held_d[n][:])
+                finish_cd(n, "s")
+            else:
+                for side, out_c in ((LEFT, "i"), (RIGHT, "j")):
+                    sub(diff_cd[n][:, side], bank[b][:, side], held_d[n][:, side])
+                    relu(res_cd[n][:, side], diff_cd[n][:, side], "s")
+                    store(out_c, n, 1, res_cd[n][:, side])
+        for b, side, out_c, terms in ((5, LEFT, "i", ("ir", "jk")), (6, RIGHT, "j", ("jr", "ki"))):
+            mm(b, side, terms[0][0], 3, terms[0][1], 1, start=True)
+            mm(b, side, terms[1][0], 3, terms[1][1], 1)
+            for q in range(2):
+                cols = slice(side.start + P * q, side.start + P * (q + 1))
+                mm(b, cols, "r", 3, out_c, 1, stop=(q == 1), skip=P * q)
+            sub(diff_cd[3][:, side], bank[b][:, side], held_d[3][:, side])
+            relu(res_cd[3][:, side], diff_cd[3][:, side], "s" if out_c == "i" else "v")
+            store(out_c, 3, 1, res_cd[3][:, side])

@@ -68,8 +68,8 @@ def tile_mix_quat_relu_kernel(
         def load_scales(c):
             for q in range(4):
                 nc.sync.dma_start(
-                    out=w_scales[c][32 * q : 32 * q + 4, :].bitcast(I32),
-                    in_=scales_hbm[c][4 * q : 4 * q + 4, :].bitcast(I32),
+                    out=w_scales[c][q:P:32, :].bitcast(I32),
+                    in_=scales_hbm[c][q:16:4, :].bitcast(I32),
                 )
 
         def interleave(c, h, on_scalar=False):
@@ -189,8 +189,6 @@ def tile_mix_quat_relu_kernel(
         quantize("k", 0)
         for a in range(2):
             lone_pair(L[a], "i", 2 * a, "k", 0)
-            if a == 1:
-                interleave("i", 1, on_scalar=True)
             hold(held_mij[a][:, :, 1, :], L[a])
             for n in (2 * a, 2 * a + 1):
                 mm(C[n], WHOLE, "r", n, "i", 0)
@@ -237,30 +235,25 @@ def tile_mix_quat_relu_kernel(
 
         interleave("r", 1)
         quantize("r", 1)
-        sub_c(0)
-        sub_c(1)
-        relu_c(0, "v")
+        interleave("i", 1, on_scalar=True)
         interleave("j", 1, on_scalar=True)
-        relu_c(1, "s")
-        store_c(0)
+        for n in range(4):
+            sub_c(n)
+            relu_c(n, "g" if n < 3 else "s")
+            if n % 2 == 1:
+                store_c(n // 2)
+        sub(diff_k[0][:], bank[KB[0]][:], held_mk[0][:])
+        finish_k(0, "s")
         quantize("i", 1)
-        sub_c(2)
-        relu_c(2, "s")
         interleave("k", 1)
         quantize("j", 1)
-        quantize("k", 1)
-        sub_c(3)
-        relu_c(3, "g")
-        store_c(1)
-        for a in range(2):
-            sub(diff_k[a][:], bank[KB[a]][:], held_mk[a][:])
-        for a in range(2):
-            sub(diff_r[a][:], held_pr[a][:], bank[L[a]][:])
 
-        def group_c(b, n):
+        def open_c(b, n):
             mm(b, LEFT, "i", n, "r", 1, start=True)
             mm(b, RIGHT, "j", n, "r", 1)
             mm(b, RIGHT, "k", n, "i", 1)
+
+        def close_c(b, n):
             mm(b, WHOLE, "r", n, "i", 1)
             mm(b, LEFT, "j", n, "k", 1, stop=True)
 
@@ -273,16 +266,16 @@ def tile_mix_quat_relu_kernel(
             mm(b, RIGHT, "i", n, "j", 1)
             mm(b, RIGHT, "k", n, "r", 1, stop=True)
 
-        def group_mk(b, n):
+        def open_b(b, n):
             mm(b, RIGHT, "j", n, "i", 1, True, True)
-
-        def group_mr(b, n):
             mm(b, LEFT, "i", n, "i", 1, start=True)
+
+        def close_b(b, n):
             mm(b, LEFT, "j", n, "j", 1)
             mm(b, LEFT, "k", n, "k", 1, stop=True)
 
         held_d = [new("held_d%d" % n) for n in range(4)]
-        held_a = [new("held_a%d" % n) for n in range(4)]
+        held_b = [new("held_b%d" % n) for n in range(4)]
         diff_cd = [new("diff_cd%d" % n) for n in range(4)]
         res_cd = [new("res_cd%d" % n) for n in range(4)]
         diff_ab = [new("diff_ab%d" % n) for n in range(4)]
@@ -293,54 +286,50 @@ def tile_mix_quat_relu_kernel(
             store("i", n, 1, res_cd[n][:, LEFT])
             store("j", n, 1, res_cd[n][:, RIGHT])
 
-        def finish_ab(n, eng):
+        def finish_ab(n, b, eng):
+            sub(diff_ab[n][:], bank[b][:], held_b[n][:])
             relu(res_ab[n][:], diff_ab[n][:], eng)
             store("r", n, 1, res_ab[n][:, LEFT])
             store("k", n, 1, res_ab[n][:, RIGHT])
 
-        def bda(n, bb, bd, ba):
-            group_mk(bb, n)
-            group_mr(bb, n)
-            hold(held_a[n][:], bb)
-            group_d(bd, n)
-            hold(held_d[n][:], bd)
-            group_a(ba, n)
-
-        def sub_ab(n, ba):
-            sub(diff_ab[n][:], bank[ba][:], held_a[n][:])
-
-        bda(0, 0, 1, 2)
-        finish_k(0, "g")
-        finish_k(1, "s")
-        finish_r(0, "g")
-        finish_r(1, "g")
-        sub_ab(0, 2)
-        bda(1, 3, 0, 4)
-        finish_ab(0, "g")
-        sub_ab(1, 4)
-        finish_ab(1, "g")
-        bda(2, 1, 5, 6)
-        sub_ab(2, 6)
-        finish_ab(2, "g")
-        bda(3, 7, 2, 3)
-        sub_ab(3, 3)
-        finish_ab(3, "s")
-        for n, b in ((0, 0), (1, 4), (2, 1)):
-            group_c(b, n)
-            if n < 2:
-                sub(diff_cd[n][:], bank[b][:], held_d[n][:])
-                finish_cd(n, "s")
-            else:
-                for side, out_c in ((LEFT, "i"), (RIGHT, "j")):
-                    sub(diff_cd[n][:, side], bank[b][:, side], held_d[n][:, side])
-                    relu(res_cd[n][:, side], diff_cd[n][:, side], "s")
-                    store(out_c, n, 1, res_cd[n][:, side])
-        for b, side, out_c, terms in ((5, LEFT, "i", ("ir", "jk")), (6, RIGHT, "j", ("jr", "ki"))):
-            mm(b, side, terms[0][0], 3, terms[0][1], 1, start=True)
-            mm(b, side, terms[1][0], 3, terms[1][1], 1)
-            for q in range(2):
-                cols = slice(side.start + P * q, side.start + P * (q + 1))
-                mm(b, cols, "r", 3, out_c, 1, stop=(q == 1), skip=P * q)
-            sub(diff_cd[3][:, side], bank[b][:, side], held_d[3][:, side])
-            relu(res_cd[3][:, side], diff_cd[3][:, side], "s" if out_c == "i" else "v")
-            store(out_c, 3, 1, res_cd[3][:, side])
+        open_c(0, 0)
+        open_c(1, 1)
+        open_b(2, 0)
+        open_b(3, 1)
+        quantize("k", 1)
+        sub(diff_k[1][:], bank[KB[1]][:], held_mk[1][:])
+        finish_k(1, "g")
+        for a in range(2):
+            sub(diff_r[a][:], held_pr[a][:], bank[L[a]][:])
+            finish_r(a, "g")
+        for n in range(2):
+            group_d(4 + n, n)
+            hold(held_d[n][:], 4 + n)
+            close_c(n, n)
+            sub(diff_cd[n][:], bank[n][:], held_d[n][:])
+            finish_cd(n, "g")
+        for n in range(2):
+            close_b(2 + n, n)
+            hold(held_b[n][:], 2 + n)
+            group_a(6 + n, n)
+            finish_ab(n, 6 + n, "g")
+        for n in range(2, 4):
+            open_b(2 + n, n)
+            close_b(2 + n, n)
+            hold(held_b[n][:], 2 + n)
+            group_a(n - 2, n)
+        finish_ab(2, 0, "v")
+        for n in range(2, 4):
+            group_d(n, n)
+            hold(held_d[n][:], n)
+        finish_ab(3, 1, "v")
+        for n, banks in ((2, (6, 0)), (3, (7, 4))):
+            for b, side, out_c, terms in ((banks[0], LEFT, "i", ("ir", "jk")), (banks[1], RIGHT, "j", ("jr", "ki"))):
+                mm(b, side, terms[0][0], n, terms[0][1], 1, start=True)
+                mm(b, side, terms[1][0], n, terms[1][1], 1)
+                for q in range(2):
+                    cols = slice(side.start + P * q, side.start + P * (q + 1))
+                    mm(b, cols, "r", n, out_c, 1, stop=(q == 1), skip=P * q)
+                sub(diff_cd[n][:, side], bank[b][:, side], held_d[n][:, side])
+                relu(res_cd[n][:, side], diff_cd[n][:, side], "v" if (n, out_c) == (3, "j") else "s")
+                store(out_c, n, 1, res_cd[n][:, side])

@@ -19,11 +19,11 @@ P = 128
 PACK = 4
 HALF = T // 2
 BANK = 512
-F32_MAX = 3.4028234663852886e38
-SLOT = {"r": 0, "k": 1, "i": 2, "j": 3}
+LONE = (6, 7)
 LEFT = slice(0, HALF)
 RIGHT = slice(HALF, BANK)
 WHOLE = slice(0, BANK)
+HALVES = (LEFT, RIGHT)
 
 
 def tile_mix_quat_relu_kernel(
@@ -52,8 +52,11 @@ def tile_mix_quat_relu_kernel(
         for c in "rijk":
             w_codes[c] = sb.tile([P, N * (2 if c == "r" else 4)], U8, name="w_codes_" + c, align_bytes=64)
             w_scales[c] = sb.tile([P, N], U8, name="w_scales_" + c, align_bytes=64)
-        x_codes = [sb.tile([P, 4 * HALF], U32, name="x_codes%d" % h, align_bytes=64) for h in range(2)]
-        x_scales = [sb.tile([P, 4 * HALF], U8, name="x_scales%d" % h, align_bytes=64) for h in range(2)]
+        x_codes = {}
+        x_scales = {}
+        for c in "rijk":
+            x_codes[c] = sb.tile([P, T], U32, name="x_codes_" + c, align_bytes=64)
+            x_scales[c] = sb.tile([P, T], U8, name="x_scales_" + c, align_bytes=64)
         raw = {}
         grouped = {}
 
@@ -74,20 +77,18 @@ def tile_mix_quat_relu_kernel(
 
         def interleave(c, h, on_scalar=False):
             grouped[c, h] = sb.tile([P, PACK * HALF], BF16, name="grouped_%s%d" % (c, h), align_bytes=64)
-            dst = grouped[c, h][:].rearrange("p (c i j) -> p c j i", i=2, j=PACK)
-            src = raw[c, h][:].rearrange("p j (c i) -> p c j i", i=2)
+            dst = grouped[c, h][:].rearrange("p (c i j) -> p c j i", i=4, j=PACK)
+            src = raw[c, h][:].rearrange("p j (c i) -> p c j i", i=4)
             if on_scalar:
                 nc.scalar.copy(out=dst, in_=src)
             else:
                 nc.vector.tensor_copy(out=dst, in_=src)
 
         def quantize(c, h):
-            cols = slice(SLOT[c] * HALF, (SLOT[c] + 1) * HALF)
-            nc.vector.quantize_mx(out=x_codes[h][:, cols].bitcast(FP8X4), scales=x_scales[h][:, cols], in_=grouped[c, h][:])
+            cols = slice(h * HALF, (h + 1) * HALF)
+            nc.vector.quantize_mx(out=x_codes[c][:, cols].bitcast(FP8X4), scales=x_scales[c][:, cols], in_=grouped[c, h][:])
 
-        def mm(b, cols, w, n, x, h, start=False, stop=False, skip=0):
-            width = cols.stop - cols.start
-            x0 = SLOT[x] * HALF + skip
+        def mm(b, cols, w, n, x, t_cols, start=False, stop=False):
             if w == "r":
                 lhs = w_codes[w][:, 2 * P * n : 2 * P * (n + 1)].bitcast(FP4X4)
             else:
@@ -96,240 +97,167 @@ def tile_mix_quat_relu_kernel(
                 out=bank[b][:, cols],
                 lhsT=lhs,
                 lhsT_scale=w_scales[w][:, P * n : P * (n + 1)],
-                rhs=x_codes[h][:, x0 : x0 + width].bitcast(FP8X4),
-                rhs_scale=x_scales[h][:, x0 : x0 + width],
+                rhs=x_codes[x][:, t_cols].bitcast(FP8X4),
+                rhs_scale=x_scales[x][:, t_cols],
                 start=start,
                 stop=stop,
             )
 
-        def lone_pair(b, w, n0, x, h):
-            mm(b, LEFT, w, n0, x, h, True, True)
-            mm(b, RIGHT, w, n0 + 1, x, h, True, True)
+        def add(b, w, n, x, cols=WHOLE, start=False, stop=False):
+            mm(b, cols, w, n, x, cols, start, stop)
 
-        def hold(dst, b, cols=WHOLE):
-            src = bank[b][:, cols]
-            if len(dst.shape) == 3:
-                src = src.rearrange("p (a t) -> p a t", a=2)
-            nc.scalar.activation(out=dst, in_=src, func=ACT.Copy)
+        held = {}
+        for name in ("pr", "mk", "mj", "pi"):
+            held[name] = [sb.tile([P, 2, T], F32, name="held_%s%d" % (name, a)) for a in range(2)]
 
-        def new(name, width=BANK):
-            fresh = sb.tile([P, width], F32, name=name)
-            return fresh
-
-        def sub(dst, plus, minus):
-            nc.vector.tensor_tensor(out=dst, in0=plus, in1=minus, op=ALU.subtract)
-
-        def relu(dst, src, eng):
-            if eng == "s":
-                nc.scalar.activation(out=dst, in_=src, func=ACT.Relu)
-            elif eng == "g":
-                nc.gpsimd.tensor_scalar(out=dst, in0=src, scalar1=F32_MAX, scalar2=0.0, op0=ALU.min, op1=ALU.max)
+        def hold_pi(n, on_vector=False):
+            if on_vector:
+                nc.vector.tensor_copy(out=held["pi"][n // 2][:, n % 2, :], in_=bank[n][:])
             else:
-                nc.vector.tensor_scalar_max(out=dst, in0=src, scalar1=0.0)
+                nc.scalar.activation(out=held["pi"][n // 2][:, n % 2, :], in_=bank[n][:], func=ACT.Copy)
 
-        def store(c, n, h, src):
-            nc.sync.dma_start(out=out_hbm[c][P * n : P * (n + 1), h * HALF : (h + 1) * HALF], in_=src)
+        HELD_OF = {"r": "pr", "i": "pi", "j": "mj", "k": "mk"}
+        diff = {}
 
-        def store_pair(c, n0, h, src):
-            rows = out_hbm[c][P * n0 : P * (n0 + 2), h * HALF : (h + 1) * HALF]
-            nc.sync.dma_start(out=rows.rearrange("(a p) t -> p a t", p=P), in_=src)
+        def sub(c, n, b, cols=WHOLE):
+            diff[c, n, cols.start] = sb.tile([P, cols.stop - cols.start], F32, name="diff_%s%d_%d" % (c, n, cols.start))
+            kept = held[HELD_OF[c]][n // 2][:, n % 2, cols]
+            if c in "ri":
+                nc.vector.tensor_tensor(out=diff[c, n, cols.start][:], in0=kept, in1=bank[b][:, cols], op=ALU.subtract)
+            else:
+                nc.vector.tensor_tensor(out=diff[c, n, cols.start][:], in0=bank[b][:, cols], in1=kept, op=ALU.subtract)
+
+        def finish(c, n, eng, cols=WHOLE):
+            res = sb.tile([P, cols.stop - cols.start], F32, name="res_%s%d_%d" % (c, n, cols.start))
+            if eng == "s":
+                nc.scalar.activation(out=res[:], in_=diff[c, n, cols.start][:], func=ACT.Relu)
+            else:
+                nc.vector.tensor_scalar_max(out=res[:], in0=diff[c, n, cols.start][:], scalar1=0.0)
+            nc.sync.dma_start(out=out_hbm[c][P * n : P * (n + 1), cols], in_=res[:])
 
         for c in "rijk":
             nc.vector.memset(w_scales[c][:].bitcast(I32), 0)
         load_x("r", 0)
         load_words("r")
         load_scales("r")
+        load_x("r", 1)
         load_words("i")
-        load_words("j")
         load_scales("i")
         load_x("i", 0)
+        load_words("j")
         load_scales("j")
-        load_words("k")
-        load_x("j", 0)
-        load_scales("k")
+        load_x("i", 1)
         load_x("k", 0)
-        for c in "rijk":
-            load_x(c, 1)
+        load_x("k", 1)
+        load_x("j", 0)
+        load_x("j", 1)
+        load_words("k")
+        load_scales("k")
 
-        C = [0, 1, 2, 3]
-        KB = [4, 5]
-        L = [6, 7]
-        held_pr = [new("held_pr%d" % a) for a in range(2)]
-        held_mk = [new("held_mk%d" % a) for a in range(2)]
-        held_mij = [sb.tile([P, 2, 2, HALF], F32, name="held_mij%d" % a) for a in range(2)]
+        def prepare(c, h):
+            interleave(c, h)
+            quantize(c, h)
 
-        interleave("r", 0)
-        quantize("r", 0)
-        for a in range(2):
-            lone_pair(L[a], "r", 2 * a, "r", 0)
-            hold(held_pr[a][:], L[a])
-        for n in range(4):
-            mm(C[n], LEFT, "i", n, "r", 0, start=True)
-        for n in range(4):
-            mm(C[n], RIGHT, "j", n, "r", 0)
-        interleave("i", 0)
-        quantize("i", 0)
-        for a in range(2):
-            lone_pair(L[a], "j", 2 * a, "i", 0)
-            hold(held_mk[a][:], L[a])
-        for a in range(2):
-            mm(KB[a], LEFT, "k", 2 * a, "r", 0, start=True)
-            mm(KB[a], RIGHT, "k", 2 * a + 1, "r", 0)
-        for n in range(4):
-            mm(C[n], RIGHT, "k", n, "i", 0)
-        interleave("j", 0)
-        quantize("j", 0)
-        for a in range(2):
-            lone_pair(L[a], "k", 2 * a, "j", 0)
-            hold(held_mij[a][:, :, 0, :], L[a])
-        for a in range(2):
-            mm(KB[a], LEFT, "i", 2 * a, "j", 0)
-            mm(KB[a], RIGHT, "i", 2 * a + 1, "j", 0)
-        interleave("k", 0)
-        quantize("k", 0)
-        for a in range(2):
-            lone_pair(L[a], "i", 2 * a, "k", 0)
-            hold(held_mij[a][:, :, 1, :], L[a])
-            for n in (2 * a, 2 * a + 1):
-                mm(C[n], WHOLE, "r", n, "i", 0)
-                mm(C[n], LEFT, "j", n, "k", 0, stop=True)
-        for a in range(2):
-            for q in range(4):
-                mm(KB[a], slice(P * q, P * (q + 1)), "r", 2 * a + q // 2, "k", 0, stop=(q == 3), skip=P * (q % 2))
-        for a in range(2):
-            for side, n in ((LEFT, 2 * a), (RIGHT, 2 * a + 1)):
-                mm(L[a], side, "i", n, "i", 0, start=True)
-                mm(L[a], side, "j", n, "j", 0)
-                mm(L[a], side, "k", n, "k", 0, stop=True)
+        def lone(name, w, x, h, a):
+            mm(LONE[a], LEFT, w, 2 * a, x, HALVES[h], True, True)
+            mm(LONE[a], RIGHT, w, 2 * a + 1, x, HALVES[h], True, True)
 
-        diff_c = [new("diff_c%d" % n) for n in range(4)]
-        res_c = [sb.tile([P, 2, 2, HALF], F32, name="res_c%d" % a) for a in range(2)]
-        diff_k = [new("diff_k%d" % a) for a in range(2)]
-        res_k = [new("res_k%d" % a) for a in range(2)]
-        diff_r = [new("diff_r%d" % a) for a in range(2)]
-        res_r = [new("res_r%d" % a) for a in range(2)]
+        def hold(name, h, a):
+            src = bank[LONE[a]][:].rearrange("p (a t) -> p a t", a=2)
+            nc.scalar.activation(out=held[name][a][:, :, HALVES[h]], in_=src, func=ACT.Copy)
 
-        def flat(ap):
-            return ap.rearrange("p a t -> p (a t)")
+        def lone_half(name, w, x, h):
+            for a in range(2):
+                lone(name, w, x, h, a)
+                hold(name, h, a)
 
-        def pair(ap):
-            return ap.rearrange("p (a t) -> p a t", a=2)
-
-        def sub_c(n):
-            sub(diff_c[n][:], bank[C[n]][:], flat(held_mij[n // 2][:, n % 2, :, :]))
-
-        def relu_c(n, eng):
-            relu(flat(res_c[n // 2][:, n % 2, :, :]), diff_c[n][:], eng)
-
-        def store_c(a):
-            store_pair("i", 2 * a, 0, res_c[a][:, :, 0, :])
-            store_pair("j", 2 * a, 0, res_c[a][:, :, 1, :])
-
-        def finish_k(a, eng):
-            relu(res_k[a][:], diff_k[a][:], eng)
-            store_pair("k", 2 * a, 0, pair(res_k[a][:]))
-
-        def finish_r(a, eng):
-            relu(res_r[a][:], diff_r[a][:], eng)
-            store_pair("r", 2 * a, 0, pair(res_r[a][:]))
-
-        interleave("r", 1)
-        quantize("r", 1)
-        interleave("i", 1, on_scalar=True)
-        interleave("j", 1, on_scalar=True)
-        for n in range(4):
-            sub_c(n)
-            relu_c(n, "g" if n < 3 else "s")
-            if n % 2 == 1:
-                store_c(n // 2)
-        sub(diff_k[0][:], bank[KB[0]][:], held_mk[0][:])
-        finish_k(0, "s")
-        quantize("i", 1)
-        interleave("k", 1)
-        quantize("j", 1)
-
-        def open_c(b, n):
-            mm(b, LEFT, "i", n, "r", 1, start=True)
-            mm(b, RIGHT, "j", n, "r", 1)
-            mm(b, RIGHT, "k", n, "i", 1)
-
-        def close_c(b, n):
-            mm(b, WHOLE, "r", n, "i", 1)
-            mm(b, LEFT, "j", n, "k", 1, stop=True)
-
-        def group_d(b, n):
-            mm(b, LEFT, "k", n, "j", 1, True, True)
-            mm(b, RIGHT, "i", n, "k", 1, True, True)
-
-        def group_a(b, n):
-            mm(b, WHOLE, "r", n, "r", 1, start=True)
-            mm(b, RIGHT, "i", n, "j", 1)
-            mm(b, RIGHT, "k", n, "r", 1, stop=True)
-
-        def open_b(b, n):
-            mm(b, RIGHT, "j", n, "i", 1, True, True)
-            mm(b, LEFT, "i", n, "i", 1, start=True)
-
-        def close_b(b, n):
-            mm(b, LEFT, "j", n, "j", 1)
-            mm(b, LEFT, "k", n, "k", 1, stop=True)
-
-        held_d = [new("held_d%d" % n) for n in range(4)]
-        held_b = [new("held_b%d" % n) for n in range(4)]
-        diff_cd = [new("diff_cd%d" % n) for n in range(4)]
-        res_cd = [new("res_cd%d" % n) for n in range(4)]
-        diff_ab = [new("diff_ab%d" % n) for n in range(4)]
-        res_ab = [new("res_ab%d" % n) for n in range(4)]
-
-        def finish_cd(n, eng):
-            relu(res_cd[n][:], diff_cd[n][:], eng)
-            store("i", n, 1, res_cd[n][:, LEFT])
-            store("j", n, 1, res_cd[n][:, RIGHT])
-
-        def finish_ab(n, b, eng):
-            sub(diff_ab[n][:], bank[b][:], held_b[n][:])
-            relu(res_ab[n][:], diff_ab[n][:], eng)
-            store("r", n, 1, res_ab[n][:, LEFT])
-            store("k", n, 1, res_ab[n][:, RIGHT])
-
-        open_c(0, 0)
-        open_c(1, 1)
-        open_b(2, 0)
-        open_b(3, 1)
-        quantize("k", 1)
-        sub(diff_k[1][:], bank[KB[1]][:], held_mk[1][:])
-        finish_k(1, "g")
-        for a in range(2):
-            sub(diff_r[a][:], held_pr[a][:], bank[L[a]][:])
-            finish_r(a, "g")
-        for n in range(2):
-            group_d(4 + n, n)
-            hold(held_d[n][:], 4 + n)
-            close_c(n, n)
-            sub(diff_cd[n][:], bank[n][:], held_d[n][:])
-            finish_cd(n, "g")
-        for n in range(2):
-            close_b(2 + n, n)
-            hold(held_b[n][:], 2 + n)
-            group_a(6 + n, n)
-            finish_ab(n, 6 + n, "g")
-        for n in range(2, 4):
-            open_b(2 + n, n)
-            close_b(2 + n, n)
-            hold(held_b[n][:], 2 + n)
-            group_a(n - 2, n)
-        finish_ab(2, 0, "v")
-        for n in range(2, 4):
-            group_d(n, n)
-            hold(held_d[n][:], n)
-        finish_ab(3, 1, "v")
-        for n, banks in ((2, (6, 0)), (3, (7, 4))):
-            for b, side, out_c, terms in ((banks[0], LEFT, "i", ("ir", "jk")), (banks[1], RIGHT, "j", ("jr", "ki"))):
-                mm(b, side, terms[0][0], n, terms[0][1], 1, start=True)
-                mm(b, side, terms[1][0], n, terms[1][1], 1)
+        def add_wr_xi(h):
+            for n in range(4):
                 for q in range(2):
-                    cols = slice(side.start + P * q, side.start + P * (q + 1))
-                    mm(b, cols, "r", n, out_c, 1, stop=(q == 1), skip=P * q)
-                sub(diff_cd[n][:, side], bank[b][:, side], held_d[n][:, side])
-                relu(res_cd[n][:, side], diff_cd[n][:, side], "v" if (n, out_c) == (3, "j") else "s")
-                store(out_c, n, 1, res_cd[n][:, side])
+                    add(n, "r", n, "i", slice(h * HALF + P * q, h * HALF + P * (q + 1)))
+
+        prepare("r", 0)
+        lone_half("pr", "r", "r", 0)
+        prepare("r", 1)
+        for n in range(4):
+            add(n, "i", n, "r", LEFT, start=True)
+        lone_half("pr", "r", "r", 1)
+        for n in range(4):
+            add(n, "i", n, "r", RIGHT)
+        prepare("i", 0)
+        for n in range(2):
+            add(4 + n, "j", n, "r", start=True)
+        lone_half("mk", "j", "i", 0)
+        add_wr_xi(0)
+        prepare("i", 1)
+        lone_half("mk", "j", "i", 1)
+        add_wr_xi(1)
+        prepare("k", 0)
+        lone_half("mj", "i", "k", 0)
+        for n in range(4):
+            add(n, "j", n, "k", LEFT)
+        prepare("k", 1)
+        for n in range(4):
+            add(n, "j", n, "k", RIGHT, stop=True)
+        for a in range(2):
+            lone("mj", "i", "k", 1, a)
+        prepare("j", 0)
+        hold_pi(0)
+        hold_pi(1)
+        hold("mj", 1, 0)
+        hold("mj", 1, 1)
+        prepare("j", 1)
+        hold_pi(2, on_vector=True)
+        hold_pi(3)
+        add(0, "r", 0, "k", start=True)
+        add(0, "i", 0, "j", LEFT)
+        add(1, "i", 0, "i", start=True)
+        add(1, "j", 0, "j", LEFT)
+        add(0, "k", 0, "r")
+
+        def mi(n, b):
+            add(b, "k", n, "j", start=True, stop=True)
+
+        def group(c, n, b, cols=WHOLE):
+            terms = {"r": ("ii", "jj", "kk"), "j": ("jr", "ki", "rj"), "k": ("rk", "ij", "kr")}[c]
+            for s, (w, x) in enumerate(terms):
+                add(b, w, n, x, cols, start=(s == 0), stop=(s == 2))
+
+        mi(0, 6)
+        sub("i", 0, 6)
+        finish("i", 0, "s")
+        add(4, "r", 0, "j")
+        add(4, "k", 0, "i", stop=True)
+        sub("j", 0, 4)
+        mi(1, 2)
+        sub("i", 1, 2)
+        finish("j", 0, "s")
+        finish("i", 1, "s")
+        add(5, "r", 1, "j")
+        add(5, "k", 1, "i", stop=True)
+        sub("j", 1, 5)
+        finish("j", 1, "s")
+        add(0, "i", 0, "j", RIGHT, stop=True)
+        sub("k", 0, 0)
+        finish("k", 0, "s")
+        add(1, "j", 0, "j", RIGHT)
+        add(1, "k", 0, "k", stop=True)
+        sub("r", 0, 1)
+        finish("r", 0, "s")
+        mi(2, 7)
+        sub("i", 2, 7)
+        finish("i", 2, "s")
+        group("j", 2, 3)
+        sub("j", 2, 3)
+        finish("j", 2, "s")
+        mi(3, 6)
+        sub("i", 3, 6)
+        finish("i", 3, "s")
+        for c, n, b in (("j", 3, 4), ("k", 1, 2), ("r", 1, 5), ("k", 2, 0), ("r", 2, 1), ("k", 3, 7)):
+            group(c, n, b)
+            sub(c, n, b)
+            finish(c, n, "s")
+        for h in range(2):
+            group("r", 3, (3, 6)[h], HALVES[h])
+            sub("r", 3, (3, 6)[h], HALVES[h])
+            finish("r", 3, "sv"[h], HALVES[h])

from contextlib import ExitStack

import concourse.mybir as mybir

K, N, T = 512, 512, 512
FLOPS = 16 * 2 * K * N * T

F32 = mybir.dt.float32
BF16 = mybir.dt.bfloat16
I32 = mybir.dt.int32
U32 = mybir.dt.uint32
U8 = mybir.dt.uint8
FP8X4 = mybir.dt.float8_e4m3fn_x4
FP4X4 = mybir.dt.float4_e2m1fn_x4
ALU = mybir.AluOpType
ACT = mybir.ActivationFunctionType

P = 128
PACK = 4
HALF = T // 2
BANK = 512
LONE = (6, 7)
LEFT = slice(0, HALF)
RIGHT = slice(HALF, BANK)
WHOLE = slice(0, BANK)
HALVES = (LEFT, RIGHT)


def tile_mix_quat_relu_kernel(
    tc, xr, xi, xj, xk, wr_words, wr_scales, wi_words, wi_scales, wj_words, wj_scales, wk_words, wk_scales,
    out_0, out_1, out_2, out_3,
):
    nc = tc.nc
    x_hbm = {"r": xr, "i": xi, "j": xj, "k": xk}
    words_hbm = {
        "r": wr_words[0],
        "i": wi_words[0].rearrange("p n t -> p (n t)"),
        "j": wj_words[0].rearrange("p n t -> p (n t)"),
        "k": wk_words[0].rearrange("p n t -> p (n t)"),
    }
    scales_hbm = {"r": wr_scales[0], "i": wi_scales[0], "j": wj_scales[0], "k": wk_scales[0]}
    out_hbm = {"r": out_0, "i": out_1, "j": out_2, "k": out_3}

    with ExitStack() as ctx:
        sb = ctx.enter_context(tc.tile_pool(name="sb", bufs=1))
        ps = ctx.enter_context(tc.psum_pool(name="ps", bufs=1))
        ctx.enter_context(tc.manual_schedule())

        bank = [ps.tile([P, BANK], F32, name="bank%d" % b) for b in range(8)]
        w_codes = {}
        w_scales = {}
        for c in "rijk":
            w_codes[c] = sb.tile([P, N * (2 if c == "r" else 4)], U8, name="w_codes_" + c, align_bytes=64)
            w_scales[c] = sb.tile([P, N], U8, name="w_scales_" + c, align_bytes=64)
        x_codes = {}
        x_scales = {}
        for c in "rijk":
            x_codes[c] = sb.tile([P, T], U32, name="x_codes_" + c, align_bytes=64)
            x_scales[c] = sb.tile([P, T], U8, name="x_scales_" + c, align_bytes=64)
        raw = {}
        grouped = {}

        def load_x(c, h):
            raw[c, h] = sb.tile([P, PACK, HALF], F32, name="raw_%s%d" % (c, h))
            cols = x_hbm[c][:, h * HALF : (h + 1) * HALF]
            nc.sync.dma_start(out=raw[c, h][:], in_=cols.rearrange("(p j) t -> p j t", j=PACK))

        def load_words(c):
            nc.sync.dma_start(out=w_codes[c][:].bitcast(I32), in_=words_hbm[c].bitcast(I32))

        def load_scales(c):
            for q in range(4):
                nc.sync.dma_start(
                    out=w_scales[c][q:P:32, :].bitcast(I32),
                    in_=scales_hbm[c][q:16:4, :].bitcast(I32),
                )

        def interleave(c, h, on_scalar=False):
            grouped[c, h] = sb.tile([P, PACK * HALF], BF16, name="grouped_%s%d" % (c, h), align_bytes=64)
            dst = grouped[c, h][:].rearrange("p (c i j) -> p c j i", i=4, j=PACK)
            src = raw[c, h][:].rearrange("p j (c i) -> p c j i", i=4)
            if on_scalar:
                nc.scalar.copy(out=dst, in_=src)
            else:
                nc.vector.tensor_copy(out=dst, in_=src)

        def quantize(c, h):
            cols = slice(h * HALF, (h + 1) * HALF)
            nc.vector.quantize_mx(out=x_codes[c][:, cols].bitcast(FP8X4), scales=x_scales[c][:, cols], in_=grouped[c, h][:])

        def mm(b, cols, w, n, x, t_cols, start=False, stop=False):
            if w == "r":
                lhs = w_codes[w][:, 2 * P * n : 2 * P * (n + 1)].bitcast(FP4X4)
            else:
                lhs = w_codes[w][:, 4 * P * n : 4 * P * (n + 1)].bitcast(FP8X4)
            nc.tensor.matmul_mx(
                out=bank[b][:, cols],
                lhsT=lhs,
                lhsT_scale=w_scales[w][:, P * n : P * (n + 1)],
                rhs=x_codes[x][:, t_cols].bitcast(FP8X4),
                rhs_scale=x_scales[x][:, t_cols],
                start=start,
                stop=stop,
            )

        def add(b, w, n, x, cols=WHOLE, start=False, stop=False):
            mm(b, cols, w, n, x, cols, start, stop)

        held = {}
        for name in ("pr", "mk", "mj", "pi"):
            held[name] = [sb.tile([P, 2, T], F32, name="held_%s%d" % (name, a)) for a in range(2)]

        def hold_pi(n, on_vector=False):
            if on_vector:
                nc.vector.tensor_copy(out=held["pi"][n // 2][:, n % 2, :], in_=bank[n][:])
            else:
                nc.scalar.activation(out=held["pi"][n // 2][:, n % 2, :], in_=bank[n][:], func=ACT.Copy)

        HELD_OF = {"r": "pr", "i": "pi", "j": "mj", "k": "mk"}
        diff = {}

        def sub(c, n, b, cols=WHOLE):
            diff[c, n, cols.start] = sb.tile([P, cols.stop - cols.start], F32, name="diff_%s%d_%d" % (c, n, cols.start))
            kept = held[HELD_OF[c]][n // 2][:, n % 2, cols]
            if c in "ri":
                nc.vector.tensor_tensor(out=diff[c, n, cols.start][:], in0=kept, in1=bank[b][:, cols], op=ALU.subtract)
            else:
                nc.vector.tensor_tensor(out=diff[c, n, cols.start][:], in0=bank[b][:, cols], in1=kept, op=ALU.subtract)

        def finish(c, n, eng, cols=WHOLE):
            res = sb.tile([P, cols.stop - cols.start], F32, name="res_%s%d_%d" % (c, n, cols.start))
            if eng == "s":
                nc.scalar.activation(out=res[:], in_=diff[c, n, cols.start][:], func=ACT.Relu)
            else:
                nc.vector.tensor_scalar_max(out=res[:], in0=diff[c, n, cols.start][:], scalar1=0.0)
            nc.sync.dma_start(out=out_hbm[c][P * n : P * (n + 1), cols], in_=res[:])

        for c in "rijk":
            nc.vector.memset(w_scales[c][:].bitcast(I32), 0)
        load_x("r", 0)
        load_words("r")
        load_scales("r")
        load_x("r", 1)
        load_words("i")
        load_scales("i")
        load_x("i", 0)
        load_words("j")
        load_scales("j")
        load_x("i", 1)
        load_x("k", 0)
        load_x("k", 1)
        load_x("j", 0)
        load_x("j", 1)
        load_words("k")
        load_scales("k")

        def prepare(c, h):
            interleave(c, h)
            quantize(c, h)

        def lone(name, w, x, h, a):
            mm(LONE[a], LEFT, w, 2 * a, x, HALVES[h], True, True)
            mm(LONE[a], RIGHT, w, 2 * a + 1, x, HALVES[h], True, True)

        def hold(name, h, a):
            src = bank[LONE[a]][:].rearrange("p (a t) -> p a t", a=2)
            nc.scalar.activation(out=held[name][a][:, :, HALVES[h]], in_=src, func=ACT.Copy)

        def lone_half(name, w, x, h):
            for a in range(2):
                lone(name, w, x, h, a)
                hold(name, h, a)

        def add_wr_xi(h):
            for n in range(4):
                for q in range(2):
                    add(n, "r", n, "i", slice(h * HALF + P * q, h * HALF + P * (q + 1)))

        prepare("r", 0)
        lone_half("pr", "r", "r", 0)
        prepare("r", 1)
        for n in range(4):
            add(n, "i", n, "r", LEFT, start=True)
        lone_half("pr", "r", "r", 1)
        for n in range(4):
            add(n, "i", n, "r", RIGHT)
        prepare("i", 0)
        for n in range(2):
            add(4 + n, "j", n, "r", start=True)
        lone_half("mk", "j", "i", 0)
        add_wr_xi(0)
        prepare("i", 1)
        lone_half("mk", "j", "i", 1)
        add_wr_xi(1)
        prepare("k", 0)
        lone_half("mj", "i", "k", 0)
        for n in range(4):
            add(n, "j", n, "k", LEFT)
        prepare("k", 1)
        for n in range(4):
            add(n, "j", n, "k", RIGHT, stop=True)
        for a in range(2):
            lone("mj", "i", "k", 1, a)
        prepare("j", 0)
        hold_pi(0)
        hold_pi(1)
        hold("mj", 1, 0)
        hold("mj", 1, 1)
        prepare("j", 1)
        hold_pi(2, on_vector=True)
        hold_pi(3)
        add(0, "r", 0, "k", start=True)
        add(0, "i", 0, "j", LEFT)
        add(1, "i", 0, "i", start=True)
        add(1, "j", 0, "j", LEFT)
        add(0, "k", 0, "r")

        def mi(n, b):
            add(b, "k", n, "j", start=True, stop=True)

        def group(c, n, b, cols=WHOLE):
            terms = {"r": ("ii", "jj", "kk"), "j": ("jr", "ki", "rj"), "k": ("rk", "ij", "kr")}[c]
            for s, (w, x) in enumerate(terms):
                add(b, w, n, x, cols, start=(s == 0), stop=(s == 2))

        mi(0, 6)
        sub("i", 0, 6)
        finish("i", 0, "s")
        add(4, "r", 0, "j")
        add(4, "k", 0, "i", stop=True)
        sub("j", 0, 4)
        mi(1, 2)
        sub("i", 1, 2)
        finish("j", 0, "s")
        finish("i", 1, "s")
        add(5, "r", 1, "j")
        add(5, "k", 1, "i", stop=True)
        sub("j", 1, 5)
        finish("j", 1, "s")
        add(0, "i", 0, "j", RIGHT, stop=True)
        sub("k", 0, 0)
        finish("k", 0, "s")
        add(1, "j", 0, "j", RIGHT)
        add(1, "k", 0, "k", stop=True)
        sub("r", 0, 1)
        finish("r", 0, "s")
        mi(2, 7)
        sub("i", 2, 7)
        finish("i", 2, "s")
        group("j", 2, 3)
        sub("j", 2, 3)
        finish("j", 2, "s")
        mi(3, 6)
        sub("i", 3, 6)
        finish("i", 3, "s")
        for c, n, b in (("j", 3, 4), ("k", 1, 2), ("r", 1, 5), ("k", 2, 0), ("r", 2, 1), ("k", 3, 7)):
            group(c, n, b)
            sub(c, n, b)
            finish(c, n, "s")
        for h in range(2):
            group("r", 3, (3, 6)[h], HALVES[h])
            sub("r", 3, (3, 6)[h], HALVES[h])
            finish("r", 3, "sv"[h], HALVES[h])
